import numpy as np
CORES = [2,10,18,26,34,42,50,58,66,74,82,90,98,106,114,122,130,138,146,154,162,170,178,186,194,202,210,218,226,234,242,250]
N = 32
PERM = [[0,16],[1,17],[2,18],[3,19],[4,20],[5,21],[6,22],[7,23],[8,24],[9,25],[10,26],[11,27],[12,28],[13,29],[14,30],[15,31],[16,0],[17,1],[18,2],[19,3],[20,4],[21,5],[22,6],[23,7],[24,8],[25,9],[26,10],[27,11],[28,12],[29,13],[30,14],[31,15]]
def setup_inputs(rng):
    return {"x": rng.standard_normal((N, 128, 8), dtype=np.float32)}
def reference(x):
    y = np.empty_like(x)
    for s, d in PERM:
        y[d] = x[s]
    return {"y": y}

@@ -1,0 +1,45 @@
+SCRATCH = {
+    "send": ("dram", [128, 8], "float32"),
+    "recv": ("dram", [128, 8], "float32"),
+}
+SEMAPHORES = ["loaded", "sent", "arrived", "stored"]
+
+
+def engines(mask):
+    n = 0
+    while mask:
+        n += mask & 1
+        mask >>= 1
+    return n
+
+
+def rank_program(g, core, T, topo):
+    rank = T.rank_of(core)
+    if rank is None:
+        return
+    perm = T.tables["PERM"]
+    dsts = [T.cores[d] for s, d in perm if s == rank]
+    srcs = [T.cores[s] for s, d in perm if d == rank]
+
+    if dsts == [core]:
+        g.dma_start(T.y[:], T.x[:]).then_inc(T.sem.stored, 16)
+        g.wait_ge(T.sem.stored, 16)
+        return
+
+    sent = 0
+    if dsts:
+        g.dma_start(T.send[:], T.x[:]).then_inc(T.sem.loaded, 16)
+        g.wait_ge(T.sem.loaded, 16)
+        for dst in dsts:
+            rid, pid = topo.addr(dst, core)
+            m = topo.mask(core, dst)
+            g.remote_dma(T.recv[:], T.send[:], T.sem.arrived, T.sem.sent, pid, rid, m)
+            sent += engines(m)
+
+    if srcs:
+        g.wait_ge(T.sem.arrived, engines(topo.mask(srcs[0], core)))
+        g.dma_start(T.y[:], T.recv[:]).then_inc(T.sem.stored, 16)
+    if sent:
+        g.wait_ge(T.sem.sent, sent)
+    if srcs:
+        g.wait_ge(T.sem.stored, 16)

@@ -4,13 +4,8 @@ SCRATCH = {
 }
 SEMAPHORES = ["loaded", "sent", "arrived", "stored"]
 
-
-def engines(mask):
-    n = 0
-    while mask:
-        n += mask & 1
-        mask >>= 1
-    return n
+NENG = 8
+MASK = (1 << NENG) - 1
 
 
 def rank_program(g, core, T, topo):
@@ -32,12 +27,11 @@ def rank_program(g, core, T, topo):
         g.wait_ge(T.sem.loaded, 16)
         for dst in dsts:
             rid, pid = topo.addr(dst, core)
-            m = topo.mask(core, dst)
-            g.remote_dma(T.recv[:], T.send[:], T.sem.arrived, T.sem.sent, pid, rid, m)
-            sent += engines(m)
+            g.remote_dma(T.recv[:], T.send[:], T.sem.arrived, T.sem.sent, pid, rid, MASK)
+            sent += NENG
 
     if srcs:
-        g.wait_ge(T.sem.arrived, engines(topo.mask(srcs[0], core)))
+        g.wait_ge(T.sem.arrived, NENG)
         g.dma_start(T.y[:], T.recv[:]).then_inc(T.sem.stored, 16)
     if sent:
         g.wait_ge(T.sem.sent, sent)

SCRATCH = {
    "send": ("dram", [128, 8], "float32"),
    "recv": ("dram", [128, 8], "float32"),
}
SEMAPHORES = ["loaded", "sent", "arrived", "stored"]

NENG = 8
MASK = (1 << NENG) - 1


def rank_program(g, core, T, topo):
    rank = T.rank_of(core)
    if rank is None:
        return
    perm = T.tables["PERM"]
    dsts = [T.cores[d] for s, d in perm if s == rank]
    srcs = [T.cores[s] for s, d in perm if d == rank]

    if dsts == [core]:
        g.dma_start(T.y[:], T.x[:]).then_inc(T.sem.stored, 16)
        g.wait_ge(T.sem.stored, 16)
        return

    sent = 0
    if dsts:
        g.dma_start(T.send[:], T.x[:]).then_inc(T.sem.loaded, 16)
        g.wait_ge(T.sem.loaded, 16)
        for dst in dsts:
            rid, pid = topo.addr(dst, core)
            g.remote_dma(T.recv[:], T.send[:], T.sem.arrived, T.sem.sent, pid, rid, MASK)
            sent += NENG

    if srcs:
        g.wait_ge(T.sem.arrived, NENG)
        g.dma_start(T.y[:], T.recv[:]).then_inc(T.sem.stored, 16)
    if sent:
        g.wait_ge(T.sem.sent, sent)
    if srcs:
        g.wait_ge(T.sem.stored, 16)
